import numpy as np
import ml_dtypes


def mxq(x, axis, fmt="e4m3"):
    dtype, down = {"e4m3": (ml_dtypes.float8_e4m3fn, 7), "e5m2": (ml_dtypes.float8_e5m2, 14)}[fmt]
    v = np.moveaxis(np.asarray(x, np.float32).astype(ml_dtypes.bfloat16).astype(np.float64), axis, -1)
    blocks = v.reshape(v.shape[:-1] + (-1, 32))
    amax = np.abs(blocks).max(-1, keepdims=True)
    byte = np.maximum(np.where(amax > 0, np.frexp(amax)[1] - 1 + 127, 0) - down, 1)
    scale = np.exp2(byte - 127.0)
    codes = (blocks / scale).astype(np.float32).astype(dtype).astype(np.float64)
    return np.moveaxis((codes * scale).reshape(v.shape), -1, axis)


WIDE = False


def mx_kscale(k):
    if not WIDE:
        return np.ones(k)
    levels = np.array([24, -24, 12, -12, 0])
    if k % 512:
        return np.exp2(np.random.permutation(np.resize(levels, k // 32))).repeat(32)
    a = np.empty((k // 512, 16))
    for p in range(k // 512):
        a[p, :8] = np.random.permutation(np.resize(levels, 8))
        for g in range(8):
            far = levels[np.abs(levels - a[p, g]) >= 10]
            a[p, g + 8] = far[np.random.randint(len(far))]
    return np.exp2(a.ravel()).repeat(32)


def f64(x):
    return np.asarray(x).astype(np.float64)


def striped8(idx):
    return np.concatenate([v.reshape(-1, 16).T for v in idx]).astype(np.uint16)


def unstriped8(offs):
    return np.stack([offs[16 * g:16 * g + 16].T.reshape(-1) for g in range(8)]).astype(np.int64)


K, L, N, T, J = 1024, 512, 512, 2048, 1024


def setup_inputs():
    n = np.random.standard_normal
    s = mx_kscale(K)[:, None]
    s2 = mx_kscale(L)[:, None]
    return {
        "xT": (n((K, T)) * s).astype(np.float32),
        "wgt": np.repeat(np.random.uniform(0.5, 2.0, (8, J)), 16, axis=0).astype(np.float32),
        "wt": (n((K, N)) / np.sqrt(K) / s).astype(np.float32),
        "c": (n((L, J)) * s2).astype(np.float32),
        "wx": (n((L, N)) / np.sqrt(L) / s2).astype(np.float32),
        "b": (0.3 * n(N)).astype(np.float32),
        "offs": striped8(np.stack([np.random.permutation(T)[:J] for _ in range(8)])),
    }


def reference(xT, wgt, wt, c, wx, b, offs):
    idx = unstriped8(offs)
    rows = np.arange(K)
    xg = f64(wgt)[rows // 4 % 128] * f64(xT)[rows[:, None], idx[rows % 512 // 64]]
    xT_ = mxq(xg, 0, "e4m3")
    wt_q_ = mxq(f64(wt), 0, "e4m3")
    wt_r_ = mxq(f64(wt) - wt_q_, 0, "e4m3")
    c_ = mxq(f64(c), 0, "e4m3")
    wx_ = mxq(f64(wx), 0, "e4m3")
    y = wt_q_.T @ xT_ + wt_r_.T @ xT_ + wx_.T @ c_
    return y + f64(b)[:, None]

@@ -1,0 +1,200 @@
+from contextlib import ExitStack
+
+import concourse.mybir as mybir
+from concourse.masks import make_identity
+
+K, L, N, T, J = 1024, 512, 512, 2048, 1024
+FLOPS = 2 * (2 * K + L) * N * J + 2 * K * N * 512
+
+F32 = mybir.dt.float32
+BF16 = mybir.dt.bfloat16
+U32 = mybir.dt.uint32
+I32 = mybir.dt.int32
+U16 = mybir.dt.uint16
+U8 = mybir.dt.uint8
+FP8X4 = mybir.dt.float8_e4m3fn_x4
+ALU = mybir.AluOpType
+IDENTITY = mybir.ActivationFunctionType.Identity
+
+P = 128
+PACK = 4
+K_PASS = P * PACK
+HALF = 256
+CHUNKS = [512,256,128,128]
+PIECES = [256,256,256,128,128]
+OWNER = [0,0,1,2,3]
+LOADS = "offs wt00 wt01 wt11 wt10 x1 c0 x2 g3 g0 x3 g1 x0 g2 x7 x4 x5 wx0 c1 wx1 x6 c4 c2 c3 g4".split()
+ORDER = "G3_2 CW10 G5_1 G7_2 G5_3 CC3 CWX1 G6_4 CW00 G0_0 G0_4 CWX0 G2_2 G2_0 QC3 G1_1 G4_1 G7_1 QWX1 G1_2 G1_3 G0_2 CW01 CC1 G4_3 QW01 G3_4 G7_3 D011 QWX0 QW00 QW10 D000 G1_0 G6_0 G7_0 QC1 CW11 G0_1 R011 CC2 G2_1 G4_0 QW11 D010 G5_0 D111 CC0 G3_1 R000 QC0 D100 D001 CX0_1 QX0_1 G3_0 R010 G6_1 CX0_2 CX0_0 CX1_0 QX0_0 QX0_2 QR01 G5_2 G4_2 Mq0_03 R001 R100 D110 QX1_0 D101 R111 G6_2 Mc_02 CX1_1 R110 Mq0_00 QC2 Mq0_01 Mr0_02 R101 Mr0_13 QR10 Mc_01 G6_3 QR00 CX1_3 Mr0_00 G0_3 Mq0_02 G1_4 Mr0_11 Mc_03 Mc_00 QX1_1 Mr0_01 CX1_2 Mq0_11 Mr0_03 QR11 Mq1_03 Mr0_10 Mr0_12 Mr1_00 Mr1_03 Mq1_02 G4_4 Mq1_00 Mr1_01 Mq0_13 G3_3 E00 Mq0_12 QX1_2 G2_3 Mq1_11 Mq1_12 CX0_3 QX1_3 Mq0_10 Mq1_01 Mr1_12 Mq1_10 Mr1_02 QX0_3 E01 E02 Mq1_13 G2_4 E03 Mc_12 Mr1_13 Mr1_10 CC4 Mr0_21 G7_4 Mr1_21 Mr1_11 Mr1_20 QC4 Mq1_21 Mq0_20 Mr0_23 Mc_11 E12 Mc_23 ST01 G5_4 Mq1_23 Mc_13 E13 Mr1_23 Mq1_20 CX0_4 ST03 Mc_21 CX1_4 Mq0_21 Mc_10 Mr1_22 QX0_4 E11 Mr0_22 QX1_4 Mr0_31 Mc_20 Mq1_22 Mc_22 E10 Mq0_22 Mr0_20 ST02 ST12 Mc_32 Mq0_31 Mq0_23 Mc_31 E21 E20 Mq1_30 Mq0_32 Mq1_32 ST21 Mr0_32 ST11 Mq1_31 ST00 E23 Mq0_33 ST20 Mr0_33 Mr1_31 Mc_30 Mr1_32 E31 Mq0_30 Mr0_30 Mr1_30 ST10 ST13 ST23 E30 E22 ST22 E32 ST31 Mq1_33 Mc_33 Mr1_33 ST32 ST30 E33 ST33".split()
+VECTOR_TASKS = "CW00 CW01 CX1_2 CC3 E02 E12 E13 E21 E20 E23 E30 E33".split()
+RUN = 4
+
+
+def runs_in(ap):
+    return ap.rearrange("p t (c i) -> p c t i", i=RUN)
+
+
+def runs_out(ap):
+    return ap.rearrange("p (c i) t -> p c t i", i=RUN)
+
+
+def tile_list_tier_bias_kernel(tc, xT, wgt, wt, c, wx, b, offs, out):
+    nc = tc.nc
+    starts = [sum(CHUNKS[:i]) for i in range(len(CHUNKS))]
+    begins = [sum(PIECES[:i]) for i in range(len(PIECES))]
+    with ExitStack() as ctx:
+        held = ctx.enter_context(tc.tile_pool(name="held", bufs=1))
+        psum = ctx.enter_context(tc.psum_pool(name="psum", bufs=1))
+
+        raw = {}
+
+        def load(name):
+            if name == "offs":
+                tile = held.tile([P, J // 16], U16, name="offsets")
+                nc.sync.dma_start(tile[:], offs)
+            elif name[0] == "x":
+                a, i = divmod(int(name[1]), PACK)
+                tile = held.tile([P, T], F32, name=name)
+                src = xT[a * K_PASS:(a + 1) * K_PASS, :].rearrange("(p i) t -> p i t", i=PACK)
+                nc.sync.dma_start(tile[:], src[:, i, :])
+            elif name[0] == "g":
+                ch = int(name[1])
+                tile = held.tile([P, PIECES[ch]], F32, name=name)
+                nc.sync.dma_start(tile[:], wgt[:, begins[ch]:begins[ch] + PIECES[ch]])
+            else:
+                if name[0] == "c":
+                    ch = int(name[1])
+                    src = c[:, begins[ch]:begins[ch] + PIECES[ch]]
+                elif name[1] == "t":
+                    a, h = int(name[2]), int(name[3])
+                    src = wt[a * K_PASS:(a + 1) * K_PASS, h * HALF:(h + 1) * HALF]
+                else:
+                    h = int(name[2])
+                    src = wx[:, h * HALF:(h + 1) * HALF]
+                tile = held.tile([P, PACK, src.shape[1]], F32, name=name)
+                nc.sync.dma_start(tile[:], src.rearrange("(p i) w -> p i w", i=PACK))
+            raw[name] = tile
+
+        for name in LOADS:
+            load(name)
+
+        rounded = {}
+        codes = {}
+        banks = {}
+
+        def cast(task, key, src):
+            tile = held.tile([P, src.shape[2], PACK], BF16, name="rounded_" + key, align_bytes=64)
+            if task in VECTOR_TASKS:
+                nc.vector.tensor_copy(out=runs_out(tile[:]), in_=runs_in(src[:]))
+            else:
+                nc.scalar.copy(out=runs_out(tile[:]), in_=runs_in(src[:]))
+            rounded[key] = tile
+
+        def quantize(key, into=None, piece=None):
+            src = rounded[key]
+            width = src.shape[1]
+            whole, first = width, 0
+            if piece is not None:
+                key = into + str(OWNER[piece])
+                whole, first = CHUNKS[OWNER[piece]], begins[piece] - starts[OWNER[piece]]
+            if key not in codes:
+                words = held.tile([P, whole], U32, name="words_" + key, align_bytes=64)
+                scales = held.tile([P, whole], U8, name="scales_" + key, align_bytes=64)
+                codes[key] = (words, scales)
+            cols = slice(first, first + width)
+            nc.vector.quantize_mx(out=codes[key][0][:, cols].bitcast(FP8X4), scales=codes[key][1][:, cols],
+                                  in_=src[:].rearrange("p w t -> p (w t)"))
+
+        def mx(dst, lhs, lcols, rhs, rcols, start, stop):
+            nc.tensor.matmul_mx(out=dst, lhsT=codes[lhs][0][:, lcols].bitcast(FP8X4), lhsT_scale=codes[lhs][1][:, lcols],
+                                rhs=codes[rhs][0][:, rcols].bitcast(FP8X4), rhs_scale=codes[rhs][1][:, rcols],
+                                start=start, stop=stop)
+
+        ident = held.tile([P, P], F32, name="ident")
+        make_identity(nc, ident[:])
+        bias_rows = held.tile([P, P], F32, name="bias_rows")
+        nc.gpsimd.memset(bias_rows[:], 0.0)
+        nc.scalar.dma_start(bias_rows[0:N // P, :], b.rearrange("(u m) -> u m", m=P))
+        picks = held.tile([P, PACK * P, PACK], BF16, name="picks", align_bytes=64)
+        nc.vector.memset(picks[:].rearrange("p w t -> p (w t)").bitcast(I32), 0)
+        for t in range(PACK):
+            nc.vector.tensor_copy(out=picks[:, t * P:(t + 1) * P, t], in_=ident[:])
+        rounded["id"] = picks
+        quantize("id")
+        bias_bank = psum.tile([P, P], F32, name="bank7")
+        nc.tensor.transpose(bias_bank[:], bias_rows[:], ident[:])
+        bias = held.tile([P, N // P], F32, name="bias")
+        nc.scalar.activation(bias[:], bias_bank[:, 0:N // P], IDENTITY)
+
+        gathered = {}
+        passes_done = {}
+        staged = {}
+
+        for task in ORDER:
+            if task[0] == "G":
+                plane, ch = int(task[1]), int(task[3])
+                a, i = divmod(plane, PACK)
+                if (a, ch) not in gathered:
+                    gathered[(a, ch)] = held.tile([P, PACK, PIECES[ch]], F32, name="gathered%d%d" % (a, ch))
+                cols = slice(begins[ch] // 16, (begins[ch] + PIECES[ch]) // 16)
+                nc.vector.tensor_tensor(gathered[(a, ch)][:, i, :], raw["x%d" % plane][:].indirect(raw["offs"][:, cols]),
+                                        raw["g%d" % ch][:], ALU.mult)
+            elif task[:3] == "CWX":
+                cast(task, "wx" + task[3], raw["wx" + task[3]])
+            elif task[:3] == "QWX":
+                quantize("wx" + task[3])
+            elif task[:2] == "CW":
+                cast(task, "wq" + task[2:], raw["wt" + task[2:]])
+            elif task[:2] == "QW":
+                quantize("wq" + task[2:])
+            elif task[:2] == "QR":
+                quantize("wr" + task[2:])
+            elif task[:2] == "CX":
+                cast(task, "x" + task[2:], gathered[(int(task[2]), int(task[4]))])
+            elif task[:2] == "QX":
+                quantize("x" + task[2:], "x" + task[2:4], int(task[4]))
+            elif task[:2] == "CC":
+                cast(task, "c" + task[2], raw["c" + task[2]])
+            elif task[:2] == "QC":
+                quantize("c" + task[2], "cq", int(task[2]))
+            elif task[0] == "D":
+                u = int(task[3])
+                bank = psum.tile([P, PACK, P], F32, name="bank%d" % (4 + 2 * int(task[2]) + u))
+                for t in range(PACK):
+                    mx(bank[:, t, :], "id", slice(t * P, (t + 1) * P), "wq" + task[1:3], slice(u * P, (u + 1) * P), True, True)
+                banks[task[1:]] = bank
+            elif task[0] == "R":
+                u = int(task[3])
+                key = "wr" + task[1:3]
+                if key not in rounded:
+                    rounded[key] = held.tile([P, HALF, PACK], BF16, name="rounded_" + key, align_bytes=64)
+                cols = slice(u * P, (u + 1) * P)
+                nc.vector.tensor_tensor(runs_out(rounded[key][:, cols, :]), runs_in(raw["wt" + task[1:3]][:, :, cols]),
+                                        runs_in(banks[task[1:]][:]), ALU.subtract)
+            elif task[0] == "M":
+                kind, where = task[1:].split("_")
+                ch, u = int(where[0]), int(where[1])
+                if where not in passes_done:
+                    passes_done[where] = 0
+                    banks["out" + where] = psum.tile([P, CHUNKS[ch]], F32, name="bank%d" % (ch % 2 * 4 + u))
+                h, v = divmod(u, 2)
+                if kind == "c":
+                    lhs, rhs = "wx%d" % h, "cq%d" % ch
+                else:
+                    lhs, rhs = "w%s%s%d" % (kind[0], kind[1], h), "x%s_%d" % (kind[1], ch)
+                passes_done[where] += 1
+                mx(banks["out" + where][:], lhs, slice(v * P, (v + 1) * P), rhs, slice(0, CHUNKS[ch]),
+                   passes_done[where] == 1, passes_done[where] == 5)
+            elif task[0] == "E":
+                ch, u = int(task[1]), int(task[2])
+                h, v = divmod(u, 2)
+                if (ch, h) not in staged:
+                    tenant = ["wt0", "wt1", "wx", "staged3", "staged4"][ch]
+                    staged[(ch, h)] = held.tile([P, 2, CHUNKS[ch]], F32, name="%s%d" % (tenant, h))
+                tile = staged[(ch, h)][:, v, :]
+                if task in VECTOR_TASKS:
+                    nc.vector.tensor_scalar(tile, banks["out" + task[1:]][:], bias[:, u:u + 1], None, ALU.add)
+                else:
+                    nc.scalar.activation(tile, banks["out" + task[1:]][:], IDENTITY, bias=bias[:, u:u + 1])
+            else:
+                ch, u = int(task[2]), int(task[3])
+                nc.sync.dma_start(out[u * P:(u + 1) * P, starts[ch]:starts[ch] + CHUNKS[ch]], staged[(ch, u // 2)][:, u % 2, :])

@@ -23,23 +23,29 @@ HALF = 256
 CHUNKS = [512,256,128,128]
 PIECES = [256,256,256,128,128]
 OWNER = [0,0,1,2,3]
-LOADS = "offs wt00 wt01 wt11 wt10 x1 c0 x2 g3 g0 x3 g1 x0 g2 x7 x4 x5 wx0 c1 wx1 x6 c4 c2 c3 g4".split()
-ORDER = "G3_2 CW10 G5_1 G7_2 G5_3 CC3 CWX1 G6_4 CW00 G0_0 G0_4 CWX0 G2_2 G2_0 QC3 G1_1 G4_1 G7_1 QWX1 G1_2 G1_3 G0_2 CW01 CC1 G4_3 QW01 G3_4 G7_3 D011 QWX0 QW00 QW10 D000 G1_0 G6_0 G7_0 QC1 CW11 G0_1 R011 CC2 G2_1 G4_0 QW11 D010 G5_0 D111 CC0 G3_1 R000 QC0 D100 D001 CX0_1 QX0_1 G3_0 R010 G6_1 CX0_2 CX0_0 CX1_0 QX0_0 QX0_2 QR01 G5_2 G4_2 Mq0_03 R001 R100 D110 QX1_0 D101 R111 G6_2 Mc_02 CX1_1 R110 Mq0_00 QC2 Mq0_01 Mr0_02 R101 Mr0_13 QR10 Mc_01 G6_3 QR00 CX1_3 Mr0_00 G0_3 Mq0_02 G1_4 Mr0_11 Mc_03 Mc_00 QX1_1 Mr0_01 CX1_2 Mq0_11 Mr0_03 QR11 Mq1_03 Mr0_10 Mr0_12 Mr1_00 Mr1_03 Mq1_02 G4_4 Mq1_00 Mr1_01 Mq0_13 G3_3 E00 Mq0_12 QX1_2 G2_3 Mq1_11 Mq1_12 CX0_3 QX1_3 Mq0_10 Mq1_01 Mr1_12 Mq1_10 Mr1_02 QX0_3 E01 E02 Mq1_13 G2_4 E03 Mc_12 Mr1_13 Mr1_10 CC4 Mr0_21 G7_4 Mr1_21 Mr1_11 Mr1_20 QC4 Mq1_21 Mq0_20 Mr0_23 Mc_11 E12 Mc_23 ST01 G5_4 Mq1_23 Mc_13 E13 Mr1_23 Mq1_20 CX0_4 ST03 Mc_21 CX1_4 Mq0_21 Mc_10 Mr1_22 QX0_4 E11 Mr0_22 QX1_4 Mr0_31 Mc_20 Mq1_22 Mc_22 E10 Mq0_22 Mr0_20 ST02 ST12 Mc_32 Mq0_31 Mq0_23 Mc_31 E21 E20 Mq1_30 Mq0_32 Mq1_32 ST21 Mr0_32 ST11 Mq1_31 ST00 E23 Mq0_33 ST20 Mr0_33 Mr1_31 Mc_30 Mr1_32 E31 Mq0_30 Mr0_30 Mr1_30 ST10 ST13 ST23 E30 E22 ST22 E32 ST31 Mq1_33 Mc_33 Mr1_33 ST32 ST30 E33 ST33".split()
-VECTOR_TASKS = "CW00 CW01 CX1_2 CC3 E02 E12 E13 E21 E20 E23 E30 E33".split()
+GATHERS = [512,384,128]
+C_LOADS = [512,512]
+STORES = [4,2,1,1]
+RUN_RESIDUAL = 4
+LOADS = "offs wt01 wt00 wt1 x1 g0 x0 x2 x3 g1 x7 x6 c0 x4 wx x5 c1 g2".split()
+ORDER = "CC0 CW10 CW01 CW11 CW00 G4_0 G2_1 G6_1 CC1 QW01 QW11 QW00 CC2 G4_1 CWX1 G5_1 G6_2 G3_1 D010 CWX0 QC2 QC1 G5_0 R010 D011 D110 G1_0 G3_0 R011 G0_0 QC0 QR01 G7_1 D111 QW10 D000 G2_0 CX1_2 R000 D001 QWX0 G7_0 G6_0 CX0_1 G0_1 CX1_0 Mc_00 QWX1 D100 Mc_03 R001 G1_1 Mc_02 R111 CX1_1 CX0_2 CX0_0 CC3 QX1_2 QX0_2 QX0_1 R110 QX0_0 Mr0_13 QX1_0 D101 R100 Mq0_00 Mq0_01 Mq0_12 G0_2 CX1_3 QR00 G3_2 Mq0_13 Mr0_00 QX1_1 R101 QR10 Mq1_13 Mq0_02 Mr0_01 G4_2 G1_2 Mq1_00 Mq0_10 Mr0_11 QC3 QR11 Mq0_03 Mr1_00 CX0_3 QX0_3 Mc_01 G7_2 Mr0_10 Mr0_03 Mr1_03 Mr0_02 Mq1_03 Mq1_01 Mr1_01 G5_2 E00 Mq1_02 Mr1_13 Mr1_02 E03 E01 E02 Mq0_20 Mq1_10 Mr1_10 Mq0_22 Mq0_21 Mq0_11 Mq0_23 Mr0_12 Mr1_11 G2_2 QX1_3 Mq1_12 Mr1_23 Mq1_20 CX0_4 QX0_4 Mq1_22 Mr0_21 CC4 Mr0_22 Mc_13 CX1_4 Mr0_23 Mr1_12 ST03 Mc_11 Mc_12 E13 ST02 E12 Mr1_21 Mc_10 E10 Mq0_33 ST00 QX1_4 Mc_21 Mc_22 Mr0_20 Mc_23 Mq1_33 Mr1_32 Mr1_22 ST11 Mq0_32 QC4 Mq1_11 ST01 Mq1_30 Mq0_30 E11 Mc_33 Mc_32 Mq1_23 Mc_20 Mr0_33 Mq1_21 Mr1_33 Mr1_20 Mr0_30 E22 Mq1_32 Mr0_31 E20 Mc_30 Mq1_31 Mr1_30 E21 Mr1_31 Mc_31 E23 Mq0_31 ST10 E30 Mr0_32 E31 E32 E33 ST30 ST20".split()
+VECTOR_TASKS = "CW01 CW11 CW00 CX1_1 CX1_3 CX0_4 CX1_4 E20 E30 E33 E32".split()
 RUN = 4
 
 
-def runs_in(ap):
-    return ap.rearrange("p t (c i) -> p c t i", i=RUN)
+def runs_in(ap, run=RUN):
+    return ap.rearrange("p t (c i) -> p c t i", i=run)
 
 
-def runs_out(ap):
-    return ap.rearrange("p (c i) t -> p c t i", i=RUN)
+def runs_out(ap, run=RUN):
+    return ap.rearrange("p (c i) t -> p c t i", i=run)
 
 
 def tile_list_tier_bias_kernel(tc, xT, wgt, wt, c, wx, b, offs, out):
     nc = tc.nc
     starts = [sum(CHUNKS[:i]) for i in range(len(CHUNKS))]
+    g_at = [sum(GATHERS[:i]) for i in range(len(GATHERS))]
+    c_at = [sum(C_LOADS[:i]) for i in range(len(C_LOADS))]
     begins = [sum(PIECES[:i]) for i in range(len(PIECES))]
     with ExitStack() as ctx:
         held = ctx.enter_context(tc.tile_pool(name="held", bufs=1))
@@ -58,24 +64,36 @@ def tile_list_tier_bias_kernel(tc, xT, wgt, wt, c, wx, b, offs, out):
                 nc.sync.dma_start(tile[:], src[:, i, :])
             elif name[0] == "g":
                 ch = int(name[1])
-                tile = held.tile([P, PIECES[ch]], F32, name=name)
-                nc.sync.dma_start(tile[:], wgt[:, begins[ch]:begins[ch] + PIECES[ch]])
+                tile = held.tile([P, GATHERS[ch]], F32, name=name)
+                nc.sync.dma_start(tile[:], wgt[:, g_at[ch]:g_at[ch] + GATHERS[ch]])
             else:
                 if name[0] == "c":
                     ch = int(name[1])
-                    src = c[:, begins[ch]:begins[ch] + PIECES[ch]]
-                elif name[1] == "t":
-                    a, h = int(name[2]), int(name[3])
-                    src = wt[a * K_PASS:(a + 1) * K_PASS, h * HALF:(h + 1) * HALF]
+                    src = c[:, c_at[ch]:c_at[ch] + C_LOADS[ch]]
+                elif name == "wx":
+                    src = wx
                 else:
-                    h = int(name[2])
-                    src = wx[:, h * HALF:(h + 1) * HALF]
+                    a = int(name[2])
+                    src = wt[a * K_PASS:(a + 1) * K_PASS, :]
+                    if len(name) == 4:
+                        h = int(name[3])
+                        src = src[:, h * HALF:(h + 1) * HALF]
                 tile = held.tile([P, PACK, src.shape[1]], F32, name=name)
                 nc.sync.dma_start(tile[:], src.rearrange("(p i) w -> p i w", i=PACK))
             raw[name] = tile
 
         for name in LOADS:
             load(name)
+
+        def half_of(name, h):
+            if name in raw:
+                return raw[name][:, :, h * HALF:(h + 1) * HALF]
+            return raw[name + str(h)][:]
+
+        def c_piece(piece):
+            k = max(i for i in range(len(C_LOADS)) if c_at[i] <= begins[piece])
+            first = begins[piece] - c_at[k]
+            return raw["c%d" % k][:, :, first:first + PIECES[piece]]
 
         rounded = {}
         codes = {}
@@ -84,9 +102,9 @@ def tile_list_tier_bias_kernel(tc, xT, wgt, wt, c, wx, b, offs, out):
         def cast(task, key, src):
             tile = held.tile([P, src.shape[2], PACK], BF16, name="rounded_" + key, align_bytes=64)
             if task in VECTOR_TASKS:
-                nc.vector.tensor_copy(out=runs_out(tile[:]), in_=runs_in(src[:]))
+                nc.vector.tensor_copy(out=runs_out(tile[:]), in_=runs_in(src))
             else:
-                nc.scalar.copy(out=runs_out(tile[:]), in_=runs_in(src[:]))
+                nc.scalar.copy(out=runs_out(tile[:]), in_=runs_in(src))
             rounded[key] = tile
 
         def quantize(key, into=None, piece=None):
@@ -134,26 +152,29 @@ def tile_list_tier_bias_kernel(tc, xT, wgt, wt, c, wx, b, offs, out):
                 plane, ch = int(task[1]), int(task[3])
                 a, i = divmod(plane, PACK)
                 if (a, ch) not in gathered:
-                    gathered[(a, ch)] = held.tile([P, PACK, PIECES[ch]], F32, name="gathered%d%d" % (a, ch))
-                cols = slice(begins[ch] // 16, (begins[ch] + PIECES[ch]) // 16)
+                    gathered[(a, ch)] = held.tile([P, PACK, GATHERS[ch]], F32, name="gathered%d%d" % (a, ch))
+                cols = slice(g_at[ch] // 16, (g_at[ch] + GATHERS[ch]) // 16)
                 nc.vector.tensor_tensor(gathered[(a, ch)][:, i, :], raw["x%d" % plane][:].indirect(raw["offs"][:, cols]),
                                         raw["g%d" % ch][:], ALU.mult)
             elif task[:3] == "CWX":
-                cast(task, "wx" + task[3], raw["wx" + task[3]])
+                cast(task, "wx" + task[3], half_of("wx", int(task[3])))
             elif task[:3] == "QWX":
                 quantize("wx" + task[3])
             elif task[:2] == "CW":
-                cast(task, "wq" + task[2:], raw["wt" + task[2:]])
+                cast(task, "wq" + task[2:], half_of("wt" + task[2], int(task[3])))
             elif task[:2] == "QW":
                 quantize("wq" + task[2:])
             elif task[:2] == "QR":
                 quantize("wr" + task[2:])
             elif task[:2] == "CX":
-                cast(task, "x" + task[2:], gathered[(int(task[2]), int(task[4]))])
+                piece = int(task[4])
+                k = max(i for i in range(len(GATHERS)) if g_at[i] <= begins[piece])
+                first = begins[piece] - g_at[k]
+                cast(task, "x" + task[2:], gathered[(int(task[2]), k)][:, :, first:first + PIECES[piece]])
             elif task[:2] == "QX":
                 quantize("x" + task[2:], "x" + task[2:4], int(task[4]))
             elif task[:2] == "CC":
-                cast(task, "c" + task[2], raw["c" + task[2]])
+                cast(task, "c" + task[2], c_piece(int(task[2])))
             elif task[:2] == "QC":
                 quantize("c" + task[2], "cq", int(task[2]))
             elif task[0] == "D":
@@ -168,8 +189,9 @@ def tile_list_tier_bias_kernel(tc, xT, wgt, wt, c, wx, b, offs, out):
                 if key not in rounded:
                     rounded[key] = held.tile([P, HALF, PACK], BF16, name="rounded_" + key, align_bytes=64)
                 cols = slice(u * P, (u + 1) * P)
-                nc.vector.tensor_tensor(runs_out(rounded[key][:, cols, :]), runs_in(raw["wt" + task[1:3]][:, :, cols]),
-                                        runs_in(banks[task[1:]][:]), ALU.subtract)
+                nc.vector.tensor_tensor(runs_out(rounded[key][:, cols, :], RUN_RESIDUAL),
+                                        runs_in(half_of("wt" + task[1], int(task[2]))[:, :, cols], RUN_RESIDUAL),
+                                        runs_in(banks[task[1:]][:], RUN_RESIDUAL), ALU.subtract)
             elif task[0] == "M":
                 kind, where = task[1:].split("_")
                 ch, u = int(where[0]), int(where[1])
@@ -186,15 +208,15 @@ def tile_list_tier_bias_kernel(tc, xT, wgt, wt, c, wx, b, offs, out):
                    passes_done[where] == 1, passes_done[where] == 5)
             elif task[0] == "E":
                 ch, u = int(task[1]), int(task[2])
-                h, v = divmod(u, 2)
-                if (ch, h) not in staged:
-                    tenant = ["wt0", "wt1", "wx", "staged3", "staged4"][ch]
-                    staged[(ch, h)] = held.tile([P, 2, CHUNKS[ch]], F32, name="%s%d" % (tenant, h))
-                tile = staged[(ch, h)][:, v, :]
+                if ch not in staged:
+                    staged[ch] = held.tile([P, N // P, CHUNKS[ch]], F32, name=["wt1", "wx", "staged2", "staged3", "staged4"][ch])
+                tile = staged[ch][:, u, :]
                 if task in VECTOR_TASKS:
                     nc.vector.tensor_scalar(tile, banks["out" + task[1:]][:], bias[:, u:u + 1], None, ALU.add)
                 else:
                     nc.scalar.activation(tile, banks["out" + task[1:]][:], IDENTITY, bias=bias[:, u:u + 1])
             else:
-                ch, u = int(task[2]), int(task[3])
-                nc.sync.dma_start(out[u * P:(u + 1) * P, starts[ch]:starts[ch] + CHUNKS[ch]], staged[(ch, u // 2)][:, u % 2, :])
+                ch, s = int(task[2]), int(task[3])
+                per = N // P // STORES[ch]
+                rows = out[s * per * P:(s + 1) * per * P, starts[ch]:starts[ch] + CHUNKS[ch]]
+                nc.sync.dma_start(rows.rearrange("(u p) j -> p u j", p=P), staged[ch][:, s * per:(s + 1) * per, :])

@@ -19,204 +19,177 @@ IDENTITY = mybir.ActivationFunctionType.Identity
 P = 128
 PACK = 4
 K_PASS = P * PACK
-HALF = 256
-CHUNKS = [512,256,128,128]
-PIECES = [256,256,256,128,128]
-OWNER = [0,0,1,2,3]
-GATHERS = [512,384,128]
-C_LOADS = [512,512]
-STORES = [4,2,1,1]
-RUN_RESIDUAL = 4
-LOADS = "offs wt01 wt00 wt1 x1 g0 x0 x2 x3 g1 x7 x6 c0 x4 wx x5 c1 g2".split()
-ORDER = "CC0 CW10 CW01 CW11 CW00 G4_0 G2_1 G6_1 CC1 QW01 QW11 QW00 CC2 G4_1 CWX1 G5_1 G6_2 G3_1 D010 CWX0 QC2 QC1 G5_0 R010 D011 D110 G1_0 G3_0 R011 G0_0 QC0 QR01 G7_1 D111 QW10 D000 G2_0 CX1_2 R000 D001 QWX0 G7_0 G6_0 CX0_1 G0_1 CX1_0 Mc_00 QWX1 D100 Mc_03 R001 G1_1 Mc_02 R111 CX1_1 CX0_2 CX0_0 CC3 QX1_2 QX0_2 QX0_1 R110 QX0_0 Mr0_13 QX1_0 D101 R100 Mq0_00 Mq0_01 Mq0_12 G0_2 CX1_3 QR00 G3_2 Mq0_13 Mr0_00 QX1_1 R101 QR10 Mq1_13 Mq0_02 Mr0_01 G4_2 G1_2 Mq1_00 Mq0_10 Mr0_11 QC3 QR11 Mq0_03 Mr1_00 CX0_3 QX0_3 Mc_01 G7_2 Mr0_10 Mr0_03 Mr1_03 Mr0_02 Mq1_03 Mq1_01 Mr1_01 G5_2 E00 Mq1_02 Mr1_13 Mr1_02 E03 E01 E02 Mq0_20 Mq1_10 Mr1_10 Mq0_22 Mq0_21 Mq0_11 Mq0_23 Mr0_12 Mr1_11 G2_2 QX1_3 Mq1_12 Mr1_23 Mq1_20 CX0_4 QX0_4 Mq1_22 Mr0_21 CC4 Mr0_22 Mc_13 CX1_4 Mr0_23 Mr1_12 ST03 Mc_11 Mc_12 E13 ST02 E12 Mr1_21 Mc_10 E10 Mq0_33 ST00 QX1_4 Mc_21 Mc_22 Mr0_20 Mc_23 Mq1_33 Mr1_32 Mr1_22 ST11 Mq0_32 QC4 Mq1_11 ST01 Mq1_30 Mq0_30 E11 Mc_33 Mc_32 Mq1_23 Mc_20 Mr0_33 Mq1_21 Mr1_33 Mr1_20 Mr0_30 E22 Mq1_32 Mr0_31 E20 Mc_30 Mq1_31 Mr1_30 E21 Mr1_31 Mc_31 E23 Mq0_31 ST10 E30 Mr0_32 E31 E32 E33 ST30 ST20".split()
-VECTOR_TASKS = "CW01 CW11 CW00 CX1_1 CX1_3 CX0_4 CX1_4 E20 E30 E33 E32".split()
+N_TILES = N // P
+HALF = N // 2
+LIST_ROWS = 16
 RUN = 4
 
+CHUNKS = [(0, 512), (512, 768), (768, 896), (896, 1024)]
+GATHERS = [(0, 512), (512, 896), (896, 1024)]
+C_LOADS = [(0, 512), (512, 1024)]
+STORES = [4, 2, 2, 2]
 
-def runs_in(ap, run=RUN):
-    return ap.rearrange("p t (c i) -> p c t i", i=run)
+LOADS = [
+    ("offs",), ("wt", 0, 0), ("wt", 0, 1), ("wt", 1, 0), ("x", 0, 0), ("x", 0, 1), ("wgt", 0),
+    ("x", 0, 2), ("wx", 0), ("x", 0, 3), ("wgt", 1), ("x", 1, 0), ("b",), ("x", 1, 1), ("x", 1, 2),
+    ("c", 0), ("wt", 1, 1), ("x", 1, 3), ("wx", 1), ("c", 1), ("wgt", 2),
+]
 
 
-def runs_out(ap, run=RUN):
-    return ap.rearrange("p (c i) t -> p c t i", i=run)
+def planes_view(ap, run=RUN):
+    return ap.rearrange("p t (r i) -> p r t i", i=run)
+
+
+def packed_view(ap, run=RUN):
+    return ap.rearrange("p (r i) t -> p r t i", i=run)
+
+
+def range_holding(ranges, column):
+    return max(i for i, (first, last) in enumerate(ranges) if first <= column)
 
 
 def tile_list_tier_bias_kernel(tc, xT, wgt, wt, c, wx, b, offs, out):
     nc = tc.nc
-    starts = [sum(CHUNKS[:i]) for i in range(len(CHUNKS))]
-    g_at = [sum(GATHERS[:i]) for i in range(len(GATHERS))]
-    c_at = [sum(C_LOADS[:i]) for i in range(len(C_LOADS))]
-    begins = [sum(PIECES[:i]) for i in range(len(PIECES))]
     with ExitStack() as ctx:
-        held = ctx.enter_context(tc.tile_pool(name="held", bufs=1))
+        sbuf = ctx.enter_context(tc.tile_pool(name="sbuf", bufs=1))
         psum = ctx.enter_context(tc.psum_pool(name="psum", bufs=1))
 
-        raw = {}
+        ident = sbuf.tile([P, P], F32, name="ident")
+        nc.vector.memset(ident[:], 0.0)
+        make_identity(nc, ident[:], nomemset=True)
 
-        def load(name):
-            if name == "offs":
-                tile = held.tile([P, J // 16], U16, name="offsets")
+        loaded = {}
+        for key in LOADS:
+            name = "_".join(str(part) for part in key)
+            if key[0] == "offs":
+                tile = sbuf.tile([P, J // LIST_ROWS], U16, name=name)
                 nc.sync.dma_start(tile[:], offs)
-            elif name[0] == "x":
-                a, i = divmod(int(name[1]), PACK)
-                tile = held.tile([P, T], F32, name=name)
-                src = xT[a * K_PASS:(a + 1) * K_PASS, :].rearrange("(p i) t -> p i t", i=PACK)
-                nc.sync.dma_start(tile[:], src[:, i, :])
-            elif name[0] == "g":
-                ch = int(name[1])
-                tile = held.tile([P, GATHERS[ch]], F32, name=name)
-                nc.sync.dma_start(tile[:], wgt[:, g_at[ch]:g_at[ch] + GATHERS[ch]])
+            elif key[0] == "b":
+                tile = sbuf.tile([P, P], F32, name=name)
+                nc.vector.memset(tile[:], 0.0)
+                nc.sync.dma_start(tile[0:N_TILES, :], b.rearrange("(u m) -> u m", m=P))
+            elif key[0] == "x":
+                rows = xT[key[1] * K_PASS:(key[1] + 1) * K_PASS, :].rearrange("(p t) w -> p t w", t=PACK)
+                tile = sbuf.tile([P, T], F32, name=name)
+                nc.sync.dma_start(tile[:], rows[:, key[2], :])
+            elif key[0] == "wgt":
+                first, last = GATHERS[key[1]]
+                tile = sbuf.tile([P, last - first], F32, name=name)
+                nc.sync.dma_start(tile[:], wgt[:, first:last])
             else:
-                if name[0] == "c":
-                    ch = int(name[1])
-                    src = c[:, c_at[ch]:c_at[ch] + C_LOADS[ch]]
-                elif name == "wx":
-                    src = wx
+                if key[0] == "c":
+                    rows = c[:, C_LOADS[key[1]][0]:C_LOADS[key[1]][1]]
+                elif key[0] == "wx":
+                    rows = wx[:, key[1] * HALF:(key[1] + 1) * HALF]
                 else:
-                    a = int(name[2])
-                    src = wt[a * K_PASS:(a + 1) * K_PASS, :]
-                    if len(name) == 4:
-                        h = int(name[3])
-                        src = src[:, h * HALF:(h + 1) * HALF]
-                tile = held.tile([P, PACK, src.shape[1]], F32, name=name)
-                nc.sync.dma_start(tile[:], src.rearrange("(p i) w -> p i w", i=PACK))
-            raw[name] = tile
+                    rows = wt[key[1] * K_PASS:(key[1] + 1) * K_PASS, key[2] * HALF:(key[2] + 1) * HALF]
+                tile = sbuf.tile([P, PACK, rows.shape[1]], F32, name=name)
+                nc.sync.dma_start(tile[:], rows.rearrange("(p t) w -> p t w", t=PACK))
+            loaded[key] = tile
 
-        for name in LOADS:
-            load(name)
-
-        def half_of(name, h):
-            if name in raw:
-                return raw[name][:, :, h * HALF:(h + 1) * HALF]
-            return raw[name + str(h)][:]
-
-        def c_piece(piece):
-            k = max(i for i in range(len(C_LOADS)) if c_at[i] <= begins[piece])
-            first = begins[piece] - c_at[k]
-            return raw["c%d" % k][:, :, first:first + PIECES[piece]]
-
-        rounded = {}
-        codes = {}
-        banks = {}
-
-        def cast(task, key, src):
-            tile = held.tile([P, src.shape[2], PACK], BF16, name="rounded_" + key, align_bytes=64)
-            if task in VECTOR_TASKS:
-                nc.vector.tensor_copy(out=runs_out(tile[:]), in_=runs_in(src))
+        def round_and_pack(planes, name, on_vector):
+            packed = sbuf.tile([P, planes.shape[2], PACK], BF16, name="packed_" + name, align_bytes=64)
+            if on_vector:
+                nc.vector.tensor_copy(out=packed_view(packed[:]), in_=planes_view(planes))
             else:
-                nc.scalar.copy(out=runs_out(tile[:]), in_=runs_in(src))
-            rounded[key] = tile
+                nc.scalar.copy(out=packed_view(packed[:]), in_=planes_view(planes))
+            return packed
 
-        def quantize(key, into=None, piece=None):
-            src = rounded[key]
-            width = src.shape[1]
-            whole, first = width, 0
-            if piece is not None:
-                key = into + str(OWNER[piece])
-                whole, first = CHUNKS[OWNER[piece]], begins[piece] - starts[OWNER[piece]]
-            if key not in codes:
-                words = held.tile([P, whole], U32, name="words_" + key, align_bytes=64)
-                scales = held.tile([P, whole], U8, name="scales_" + key, align_bytes=64)
-                codes[key] = (words, scales)
-            cols = slice(first, first + width)
-            nc.vector.quantize_mx(out=codes[key][0][:, cols].bitcast(FP8X4), scales=codes[key][1][:, cols],
-                                  in_=src[:].rearrange("p w t -> p (w t)"))
+        def quantize(packed, name, codes_name):
+            width = packed.shape[1]
+            codes = sbuf.tile([P, width], U32, name=codes_name, align_bytes=64)
+            scales = sbuf.tile([P, width], U8, name="scales_" + name, align_bytes=64)
+            nc.vector.quantize_mx(out=codes[:].bitcast(FP8X4), scales=scales[:],
+                                  in_=packed[:].rearrange("p w t -> p (w t)"))
+            return codes, scales
 
-        def mx(dst, lhs, lcols, rhs, rcols, start, stop):
-            nc.tensor.matmul_mx(out=dst, lhsT=codes[lhs][0][:, lcols].bitcast(FP8X4), lhsT_scale=codes[lhs][1][:, lcols],
-                                rhs=codes[rhs][0][:, rcols].bitcast(FP8X4), rhs_scale=codes[rhs][1][:, rcols],
+        def operand(planes, name, on_vector=False):
+            return quantize(round_and_pack(planes, name, on_vector), name, "codes_" + name)
+
+        def multiply(dst, lhs, lhs_cols, rhs, rhs_cols, start, stop):
+            nc.tensor.matmul_mx(out=dst, lhsT=lhs[0][:, lhs_cols].bitcast(FP8X4), lhsT_scale=lhs[1][:, lhs_cols],
+                                rhs=rhs[0][:, rhs_cols].bitcast(FP8X4), rhs_scale=rhs[1][:, rhs_cols],
                                 start=start, stop=stop)
 
-        ident = held.tile([P, P], F32, name="ident")
-        make_identity(nc, ident[:])
-        bias_rows = held.tile([P, P], F32, name="bias_rows")
-        nc.gpsimd.memset(bias_rows[:], 0.0)
-        nc.scalar.dma_start(bias_rows[0:N // P, :], b.rearrange("(u m) -> u m", m=P))
-        picks = held.tile([P, PACK * P, PACK], BF16, name="picks", align_bytes=64)
-        nc.vector.memset(picks[:].rearrange("p w t -> p (w t)").bitcast(I32), 0)
+        one_hot = []
         for t in range(PACK):
-            nc.vector.tensor_copy(out=picks[:, t * P:(t + 1) * P, t], in_=ident[:])
-        rounded["id"] = picks
-        quantize("id")
-        bias_bank = psum.tile([P, P], F32, name="bank7")
-        nc.tensor.transpose(bias_bank[:], bias_rows[:], ident[:])
-        bias = held.tile([P, N // P], F32, name="bias")
-        nc.scalar.activation(bias[:], bias_bank[:, 0:N // P], IDENTITY)
+            tile = sbuf.tile([P, P, PACK], BF16, name="one_hot%d" % t, align_bytes=64)
+            nc.vector.memset(tile[:].rearrange("p m t -> p (m t)").bitcast(I32), 0)
+            one_hot.append(tile)
+        for t in range(PACK):
+            nc.vector.tensor_copy(out=one_hot[t][:, :, t], in_=ident[:])
+        select = [quantize(one_hot[t], "select%d" % t, "codes_select%d" % t) for t in range(PACK)]
+
+        bias_bank = psum.tile([P, P], F32, name="bank3")
+        nc.tensor.transpose(bias_bank[:], loaded[("b",)][:], ident[:])
+        bias = sbuf.tile([P, N_TILES], F32, name="bias")
+        nc.scalar.activation(bias[:], bias_bank[:, 0:N_TILES], IDENTITY)
+
+        wt_q, wt_r, wx_q = {}, {}, {}
+        for a in range(K // K_PASS):
+            for h in range(2):
+                name = "wt%d%d" % (a, h)
+                planes = loaded[("wt", a, h)]
+                packed = round_and_pack(planes[:], name, (a, h) == (0, 0))
+                wt_q[(a, h)] = quantize(packed, name, "one_hot%d" % (2 * a + h))
+                values = []
+                for v in range(2):
+                    bank = psum.tile([P, PACK, P], F32, name="bank%d" % (N_TILES + 2 * h + v))
+                    for t in range(PACK):
+                        multiply(bank[:, t, :], select[t], slice(0, P), wt_q[(a, h)],
+                                 slice(v * P, (v + 1) * P), True, True)
+                    values.append(bank)
+                rest = sbuf.tile([P, HALF, PACK], BF16, name="rest_" + name, align_bytes=64)
+                for v in range(2):
+                    cols = slice(v * P, (v + 1) * P)
+                    nc.vector.tensor_tensor(packed_view(rest[:, cols, :]), planes_view(planes[:, :, cols]),
+                                            planes_view(values[v][:]), ALU.subtract)
+                wt_r[(a, h)] = quantize(rest, "rest_" + name, "codes_rest_" + name)
+        for h in range(2):
+            wx_q[h] = operand(loaded[("wx", h)][:], "wx%d" % h)
+
+        c_q = []
+        for chunk, (first, last) in enumerate(CHUNKS):
+            part = range_holding(C_LOADS, first)
+            at = C_LOADS[part][0]
+            c_q.append(operand(loaded[("c", part)][:, :, first - at:last - at], "c%d" % chunk,
+                               on_vector=part == len(C_LOADS) - 1))
 
         gathered = {}
-        passes_done = {}
-        staged = {}
+        for chunk, (first, last) in enumerate(CHUNKS):
+            width = last - first
+            part = range_holding(GATHERS, first)
+            at, end = GATHERS[part]
+            if at == first:
+                offsets = loaded[("offs",)][:, at // LIST_ROWS:end // LIST_ROWS]
+                for a in range(K // K_PASS):
+                    picked = sbuf.tile([P, PACK, end - at], F32, name="picked%d%d" % (a, part))
+                    for t in range(PACK):
+                        nc.vector.tensor_tensor(picked[:, t, :], loaded[("x", a, t)][:].indirect(offsets),
+                                                loaded[("wgt", part)][:], ALU.mult)
+                    gathered[(a, part)] = picked
+            xg_q = [operand(gathered[(a, part)][:, :, first - at:last - at], "xg%d%d" % (a, chunk))
+                    for a in range(K // K_PASS)]
 
-        for task in ORDER:
-            if task[0] == "G":
-                plane, ch = int(task[1]), int(task[3])
-                a, i = divmod(plane, PACK)
-                if (a, ch) not in gathered:
-                    gathered[(a, ch)] = held.tile([P, PACK, GATHERS[ch]], F32, name="gathered%d%d" % (a, ch))
-                cols = slice(g_at[ch] // 16, (g_at[ch] + GATHERS[ch]) // 16)
-                nc.vector.tensor_tensor(gathered[(a, ch)][:, i, :], raw["x%d" % plane][:].indirect(raw["offs"][:, cols]),
-                                        raw["g%d" % ch][:], ALU.mult)
-            elif task[:3] == "CWX":
-                cast(task, "wx" + task[3], half_of("wx", int(task[3])))
-            elif task[:3] == "QWX":
-                quantize("wx" + task[3])
-            elif task[:2] == "CW":
-                cast(task, "wq" + task[2:], half_of("wt" + task[2], int(task[3])))
-            elif task[:2] == "QW":
-                quantize("wq" + task[2:])
-            elif task[:2] == "QR":
-                quantize("wr" + task[2:])
-            elif task[:2] == "CX":
-                piece = int(task[4])
-                k = max(i for i in range(len(GATHERS)) if g_at[i] <= begins[piece])
-                first = begins[piece] - g_at[k]
-                cast(task, "x" + task[2:], gathered[(int(task[2]), k)][:, :, first:first + PIECES[piece]])
-            elif task[:2] == "QX":
-                quantize("x" + task[2:], "x" + task[2:4], int(task[4]))
-            elif task[:2] == "CC":
-                cast(task, "c" + task[2], c_piece(int(task[2])))
-            elif task[:2] == "QC":
-                quantize("c" + task[2], "cq", int(task[2]))
-            elif task[0] == "D":
-                u = int(task[3])
-                bank = psum.tile([P, PACK, P], F32, name="bank%d" % (4 + 2 * int(task[2]) + u))
-                for t in range(PACK):
-                    mx(bank[:, t, :], "id", slice(t * P, (t + 1) * P), "wq" + task[1:3], slice(u * P, (u + 1) * P), True, True)
-                banks[task[1:]] = bank
-            elif task[0] == "R":
-                u = int(task[3])
-                key = "wr" + task[1:3]
-                if key not in rounded:
-                    rounded[key] = held.tile([P, HALF, PACK], BF16, name="rounded_" + key, align_bytes=64)
-                cols = slice(u * P, (u + 1) * P)
-                nc.vector.tensor_tensor(runs_out(rounded[key][:, cols, :], RUN_RESIDUAL),
-                                        runs_in(half_of("wt" + task[1], int(task[2]))[:, :, cols], RUN_RESIDUAL),
-                                        runs_in(banks[task[1:]][:], RUN_RESIDUAL), ALU.subtract)
-            elif task[0] == "M":
-                kind, where = task[1:].split("_")
-                ch, u = int(where[0]), int(where[1])
-                if where not in passes_done:
-                    passes_done[where] = 0
-                    banks["out" + where] = psum.tile([P, CHUNKS[ch]], F32, name="bank%d" % (ch % 2 * 4 + u))
+            sums = [psum.tile([P, width], F32, name="bank%d" % (chunk % 2 * N_TILES + u)) for u in range(N_TILES)]
+            early = [(lambda h: wt_q[(0, h)], xg_q[0]), (lambda h: wt_r[(0, h)], xg_q[0]), (wx_q.get, c_q[chunk])]
+            late = [(lambda h: wt_q[(1, h)], xg_q[1]), (lambda h: wt_r[(1, h)], xg_q[1])]
+            order = [(i, u) for i in range(len(early)) for u in range(N_TILES)]
+            order += [(len(early) + i, u) for u in range(N_TILES) for i in range(len(late))]
+            passes = early + late
+            for i, u in order:
                 h, v = divmod(u, 2)
-                if kind == "c":
-                    lhs, rhs = "wx%d" % h, "cq%d" % ch
+                multiply(sums[u][:], passes[i][0](h), slice(v * P, (v + 1) * P), passes[i][1], slice(0, width),
+                         i == 0, i == len(passes) - 1)
+
+            result = sbuf.tile([P, N_TILES, width], F32, name=["wt_1_0", "wx_0", "result2", "result3"][chunk])
+            per_store = N_TILES // STORES[chunk]
+            for u in range(N_TILES):
+                if chunk > 0 and u % 2 == 1:
+                    nc.vector.tensor_scalar(result[:, u, :], sums[u][:], bias[:, u:u + 1], None, ALU.add)
                 else:
-                    lhs, rhs = "w%s%s%d" % (kind[0], kind[1], h), "x%s_%d" % (kind[1], ch)
-                passes_done[where] += 1
-                mx(banks["out" + where][:], lhs, slice(v * P, (v + 1) * P), rhs, slice(0, CHUNKS[ch]),
-                   passes_done[where] == 1, passes_done[where] == 5)
-            elif task[0] == "E":
-                ch, u = int(task[1]), int(task[2])
-                if ch not in staged:
-                    staged[ch] = held.tile([P, N // P, CHUNKS[ch]], F32, name=["wt1", "wx", "staged2", "staged3", "staged4"][ch])
-                tile = staged[ch][:, u, :]
-                if task in VECTOR_TASKS:
-                    nc.vector.tensor_scalar(tile, banks["out" + task[1:]][:], bias[:, u:u + 1], None, ALU.add)
-                else:
-                    nc.scalar.activation(tile, banks["out" + task[1:]][:], IDENTITY, bias=bias[:, u:u + 1])
-            else:
-                ch, s = int(task[2]), int(task[3])
-                per = N // P // STORES[ch]
-                rows = out[s * per * P:(s + 1) * per * P, starts[ch]:starts[ch] + CHUNKS[ch]]
-                nc.sync.dma_start(rows.rearrange("(u p) j -> p u j", p=P), staged[ch][:, s * per:(s + 1) * per, :])
+                    nc.scalar.activation(result[:, u, :], sums[u][:], IDENTITY, bias=bias[:, u:u + 1])
+                if (u + 1) % per_store == 0:
+                    tiles = slice(u + 1 - per_store, u + 1)
+                    rows = out[tiles.start * P:tiles.stop * P, first:last]
+                    nc.sync.dma_start(rows.rearrange("(u p) j -> p u j", p=P), result[:, tiles, :])

@@ -30,9 +30,9 @@ C_LOADS = [(0, 512), (512, 1024)]
 STORES = [4, 2, 2, 2]
 
 LOADS = [
-    ("offs",), ("wt", 0, 0), ("wt", 0, 1), ("wt", 1, 0), ("x", 0, 0), ("x", 0, 1), ("wgt", 0),
-    ("x", 0, 2), ("wx", 0), ("x", 0, 3), ("wgt", 1), ("x", 1, 0), ("b",), ("x", 1, 1), ("x", 1, 2),
-    ("c", 0), ("wt", 1, 1), ("x", 1, 3), ("wx", 1), ("c", 1), ("wgt", 2),
+    ("offs",), ("wt", 0, 0), ("wt", 0, 1), ("wt", 1, 0), ("b",), ("x", 0, 0), ("x", 0, 1), ("wgt", 0),
+    ("x", 0, 2), ("x", 0, 3), ("wgt", 1), ("x", 1, 0), ("x", 1, 1), ("x", 1, 2), ("c", 0),
+    ("wt", 1, 1), ("x", 1, 3), ("wx", 0), ("wx", 1), ("c", 1), ("wgt", 2),
 ]
 
 
@@ -146,7 +146,7 @@ def tile_list_tier_bias_kernel(tc, xT, wgt, wt, c, wx, b, offs, out):
                                             planes_view(values[v][:]), ALU.subtract)
                 wt_r[(a, h)] = quantize(rest, "rest_" + name, "codes_rest_" + name)
         for h in range(2):
-            wx_q[h] = operand(loaded[("wx", h)][:], "wx%d" % h)
+            wx_q[h] = operand(loaded[("wx", h)][:], "wx%d" % h, on_vector=h == 0)
 
         c_q = []
         for chunk, (first, last) in enumerate(CHUNKS):

from contextlib import ExitStack

import concourse.mybir as mybir
from concourse.masks import make_identity

K, L, N, T, J = 1024, 512, 512, 2048, 1024
FLOPS = 2 * (2 * K + L) * N * J + 2 * K * N * 512

F32 = mybir.dt.float32
BF16 = mybir.dt.bfloat16
U32 = mybir.dt.uint32
I32 = mybir.dt.int32
U16 = mybir.dt.uint16
U8 = mybir.dt.uint8
FP8X4 = mybir.dt.float8_e4m3fn_x4
ALU = mybir.AluOpType
IDENTITY = mybir.ActivationFunctionType.Identity

P = 128
PACK = 4
K_PASS = P * PACK
N_TILES = N // P
HALF = N // 2
LIST_ROWS = 16
RUN = 4

CHUNKS = [(0, 512), (512, 768), (768, 896), (896, 1024)]
GATHERS = [(0, 512), (512, 896), (896, 1024)]
C_LOADS = [(0, 512), (512, 1024)]
STORES = [4, 2, 2, 2]

LOADS = [
    ("offs",), ("wt", 0, 0), ("wt", 0, 1), ("wt", 1, 0), ("b",), ("x", 0, 0), ("x", 0, 1), ("wgt", 0),
    ("x", 0, 2), ("x", 0, 3), ("wgt", 1), ("x", 1, 0), ("x", 1, 1), ("x", 1, 2), ("c", 0),
    ("wt", 1, 1), ("x", 1, 3), ("wx", 0), ("wx", 1), ("c", 1), ("wgt", 2),
]


def planes_view(ap, run=RUN):
    return ap.rearrange("p t (r i) -> p r t i", i=run)


def packed_view(ap, run=RUN):
    return ap.rearrange("p (r i) t -> p r t i", i=run)


def range_holding(ranges, column):
    return max(i for i, (first, last) in enumerate(ranges) if first <= column)


def tile_list_tier_bias_kernel(tc, xT, wgt, wt, c, wx, b, offs, out):
    nc = tc.nc
    with ExitStack() as ctx:
        sbuf = ctx.enter_context(tc.tile_pool(name="sbuf", bufs=1))
        psum = ctx.enter_context(tc.psum_pool(name="psum", bufs=1))

        ident = sbuf.tile([P, P], F32, name="ident")
        nc.vector.memset(ident[:], 0.0)
        make_identity(nc, ident[:], nomemset=True)

        loaded = {}
        for key in LOADS:
            name = "_".join(str(part) for part in key)
            if key[0] == "offs":
                tile = sbuf.tile([P, J // LIST_ROWS], U16, name=name)
                nc.sync.dma_start(tile[:], offs)
            elif key[0] == "b":
                tile = sbuf.tile([P, P], F32, name=name)
                nc.vector.memset(tile[:], 0.0)
                nc.sync.dma_start(tile[0:N_TILES, :], b.rearrange("(u m) -> u m", m=P))
            elif key[0] == "x":
                rows = xT[key[1] * K_PASS:(key[1] + 1) * K_PASS, :].rearrange("(p t) w -> p t w", t=PACK)
                tile = sbuf.tile([P, T], F32, name=name)
                nc.sync.dma_start(tile[:], rows[:, key[2], :])
            elif key[0] == "wgt":
                first, last = GATHERS[key[1]]
                tile = sbuf.tile([P, last - first], F32, name=name)
                nc.sync.dma_start(tile[:], wgt[:, first:last])
            else:
                if key[0] == "c":
                    rows = c[:, C_LOADS[key[1]][0]:C_LOADS[key[1]][1]]
                elif key[0] == "wx":
                    rows = wx[:, key[1] * HALF:(key[1] + 1) * HALF]
                else:
                    rows = wt[key[1] * K_PASS:(key[1] + 1) * K_PASS, key[2] * HALF:(key[2] + 1) * HALF]
                tile = sbuf.tile([P, PACK, rows.shape[1]], F32, name=name)
                nc.sync.dma_start(tile[:], rows.rearrange("(p t) w -> p t w", t=PACK))
            loaded[key] = tile

        def round_and_pack(planes, name, on_vector):
            packed = sbuf.tile([P, planes.shape[2], PACK], BF16, name="packed_" + name, align_bytes=64)
            if on_vector:
                nc.vector.tensor_copy(out=packed_view(packed[:]), in_=planes_view(planes))
            else:
                nc.scalar.copy(out=packed_view(packed[:]), in_=planes_view(planes))
            return packed

        def quantize(packed, name, codes_name):
            width = packed.shape[1]
            codes = sbuf.tile([P, width], U32, name=codes_name, align_bytes=64)
            scales = sbuf.tile([P, width], U8, name="scales_" + name, align_bytes=64)
            nc.vector.quantize_mx(out=codes[:].bitcast(FP8X4), scales=scales[:],
                                  in_=packed[:].rearrange("p w t -> p (w t)"))
            return codes, scales

        def operand(planes, name, on_vector=False):
            return quantize(round_and_pack(planes, name, on_vector), name, "codes_" + name)

        def multiply(dst, lhs, lhs_cols, rhs, rhs_cols, start, stop):
            nc.tensor.matmul_mx(out=dst, lhsT=lhs[0][:, lhs_cols].bitcast(FP8X4), lhsT_scale=lhs[1][:, lhs_cols],
                                rhs=rhs[0][:, rhs_cols].bitcast(FP8X4), rhs_scale=rhs[1][:, rhs_cols],
                                start=start, stop=stop)

        one_hot = []
        for t in range(PACK):
            tile = sbuf.tile([P, P, PACK], BF16, name="one_hot%d" % t, align_bytes=64)
            nc.vector.memset(tile[:].rearrange("p m t -> p (m t)").bitcast(I32), 0)
            one_hot.append(tile)
        for t in range(PACK):
            nc.vector.tensor_copy(out=one_hot[t][:, :, t], in_=ident[:])
        select = [quantize(one_hot[t], "select%d" % t, "codes_select%d" % t) for t in range(PACK)]

        bias_bank = psum.tile([P, P], F32, name="bank3")
        nc.tensor.transpose(bias_bank[:], loaded[("b",)][:], ident[:])
        bias = sbuf.tile([P, N_TILES], F32, name="bias")
        nc.scalar.activation(bias[:], bias_bank[:, 0:N_TILES], IDENTITY)

        wt_q, wt_r, wx_q = {}, {}, {}
        for a in range(K // K_PASS):
            for h in range(2):
                name = "wt%d%d" % (a, h)
                planes = loaded[("wt", a, h)]
                packed = round_and_pack(planes[:], name, (a, h) == (0, 0))
                wt_q[(a, h)] = quantize(packed, name, "one_hot%d" % (2 * a + h))
                values = []
                for v in range(2):
                    bank = psum.tile([P, PACK, P], F32, name="bank%d" % (N_TILES + 2 * h + v))
                    for t in range(PACK):
                        multiply(bank[:, t, :], select[t], slice(0, P), wt_q[(a, h)],
                                 slice(v * P, (v + 1) * P), True, True)
                    values.append(bank)
                rest = sbuf.tile([P, HALF, PACK], BF16, name="rest_" + name, align_bytes=64)
                for v in range(2):
                    cols = slice(v * P, (v + 1) * P)
                    nc.vector.tensor_tensor(packed_view(rest[:, cols, :]), planes_view(planes[:, :, cols]),
                                            planes_view(values[v][:]), ALU.subtract)
                wt_r[(a, h)] = quantize(rest, "rest_" + name, "codes_rest_" + name)
        for h in range(2):
            wx_q[h] = operand(loaded[("wx", h)][:], "wx%d" % h, on_vector=h == 0)

        c_q = []
        for chunk, (first, last) in enumerate(CHUNKS):
            part = range_holding(C_LOADS, first)
            at = C_LOADS[part][0]
            c_q.append(operand(loaded[("c", part)][:, :, first - at:last - at], "c%d" % chunk,
                               on_vector=part == len(C_LOADS) - 1))

        gathered = {}
        for chunk, (first, last) in enumerate(CHUNKS):
            width = last - first
            part = range_holding(GATHERS, first)
            at, end = GATHERS[part]
            if at == first:
                offsets = loaded[("offs",)][:, at // LIST_ROWS:end // LIST_ROWS]
                for a in range(K // K_PASS):
                    picked = sbuf.tile([P, PACK, end - at], F32, name="picked%d%d" % (a, part))
                    for t in range(PACK):
                        nc.vector.tensor_tensor(picked[:, t, :], loaded[("x", a, t)][:].indirect(offsets),
                                                loaded[("wgt", part)][:], ALU.mult)
                    gathered[(a, part)] = picked
            xg_q = [operand(gathered[(a, part)][:, :, first - at:last - at], "xg%d%d" % (a, chunk))
                    for a in range(K // K_PASS)]

            sums = [psum.tile([P, width], F32, name="bank%d" % (chunk % 2 * N_TILES + u)) for u in range(N_TILES)]
            early = [(lambda h: wt_q[(0, h)], xg_q[0]), (lambda h: wt_r[(0, h)], xg_q[0]), (wx_q.get, c_q[chunk])]
            late = [(lambda h: wt_q[(1, h)], xg_q[1]), (lambda h: wt_r[(1, h)], xg_q[1])]
            order = [(i, u) for i in range(len(early)) for u in range(N_TILES)]
            order += [(len(early) + i, u) for u in range(N_TILES) for i in range(len(late))]
            passes = early + late
            for i, u in order:
                h, v = divmod(u, 2)
                multiply(sums[u][:], passes[i][0](h), slice(v * P, (v + 1) * P), passes[i][1], slice(0, width),
                         i == 0, i == len(passes) - 1)

            result = sbuf.tile([P, N_TILES, width], F32, name=["wt_1_0", "wx_0", "result2", "result3"][chunk])
            per_store = N_TILES // STORES[chunk]
            for u in range(N_TILES):
                if chunk > 0 and u % 2 == 1:
                    nc.vector.tensor_scalar(result[:, u, :], sums[u][:], bias[:, u:u + 1], None, ALU.add)
                else:
                    nc.scalar.activation(result[:, u, :], sums[u][:], IDENTITY, bias=bias[:, u:u + 1])
                if (u + 1) % per_store == 0:
                    tiles = slice(u + 1 - per_store, u + 1)
                    rows = out[tiles.start * P:tiles.stop * P, first:last]
                    nc.sync.dma_start(rows.rearrange("(u p) j -> p u j", p=P), result[:, tiles, :])
